import numpy as np
import ml_dtypes


def mxq(x, axis, fmt="e4m3"):
    dtype, down = {"e4m3": (ml_dtypes.float8_e4m3fn, 7), "e5m2": (ml_dtypes.float8_e5m2, 14)}[fmt]
    v = np.moveaxis(np.asarray(x, np.float32).astype(ml_dtypes.bfloat16).astype(np.float64), axis, -1)
    blocks = v.reshape(v.shape[:-1] + (-1, 32))
    amax = np.abs(blocks).max(-1, keepdims=True)
    byte = np.maximum(np.where(amax > 0, np.frexp(amax)[1] - 1 + 127, 0) - down, 1)
    scale = np.exp2(byte - 127.0)
    codes = (blocks / scale).astype(np.float32).astype(dtype).astype(np.float64)
    return np.moveaxis((codes * scale).reshape(v.shape), -1, axis)


WIDE = False


def mx_kscale(k):
    if not WIDE:
        return np.ones(k)
    levels = np.array([10, -10, 5, -5, 0])
    if k % 512:
        return np.exp2(np.random.permutation(np.resize(levels, k // 32))).repeat(32)
    a = np.empty((k // 512, 16))
    for p in range(k // 512):
        a[p, :8] = np.random.permutation(np.resize(levels, 8))
        for g in range(8):
            far = levels[np.abs(levels - a[p, g]) >= 10]
            a[p, g + 8] = far[np.random.randint(len(far))]
    return np.exp2(a.ravel()).repeat(32)


BF16 = ml_dtypes.bfloat16


def bf(x):
    return np.asarray(x, np.float32).astype(BF16)


def f64(x):
    return np.asarray(x).astype(np.float64)


E2M1 = np.array([0.0, 0.5, 1.0, 1.5, 2.0, 3.0, 4.0, 6.0, -0.0, -0.5, -1.0, -1.5, -2.0, -3.0, -4.0, -6.0])


def pack_weight(w, fmt):
    k, n = w.shape
    w = f64(bf(w)).reshape(k // 32, 32, n)
    amax = np.abs(w).max(1)
    if fmt == "e4m3":
        byte = np.frexp(amax)[1] - 1 + 127 - 7
    else:
        mant, ex = np.frexp(amax / 6.0)
        byte = np.where(mant > 0.5, ex, ex - 1) + 127
    byte = np.clip(np.where(amax > 0, byte, 1), 1, 254)
    scaled = (w * np.exp2(127.0 - byte)[:, None, :]).reshape(k, n).astype(np.float32)
    by_word = np.ascontiguousarray(scaled.reshape(k // 512, 128, 4, n).transpose(0, 1, 3, 2))
    if fmt == "e4m3":
        words = by_word.astype(ml_dtypes.float8_e4m3fn).view(np.uint8)
    else:
        c = by_word.astype(ml_dtypes.float4_e2m1fn).view(np.uint8) & 0xF
        words = c[..., 0::2] | (c[..., 1::2] << 4)
    return np.ascontiguousarray(words), np.ascontiguousarray(byte.astype(np.uint8).reshape(k // 512, 16, n))


def unpack_weight(words, scales, fmt):
    g, p, n, _ = words.shape
    if fmt == "e4m3":
        vals = np.ascontiguousarray(words).view(ml_dtypes.float8_e4m3fn).astype(np.float64)
    else:
        nib = np.empty((g, p, n, 4), np.uint8)
        nib[..., 0::2] = words & 0xF
        nib[..., 1::2] = words >> 4
        vals = E2M1[nib]
    vals = vals * np.repeat(np.exp2(scales.astype(np.float64) - 127.0), 8, axis=1)[..., None]
    return vals.transpose(0, 1, 3, 2).reshape(g * 512, n)
def pack4(w):
    words, scales = pack_weight(w, "e2m1")
    return words.reshape(words.shape[0], 128, -1), scales


def unpack4(words, scales):
    return unpack_weight(words.reshape(words.shape[0], 128, -1, 2), scales, "e2m1")


M, K, F, N = 1024, 2048, 1024, 1536

STEEPNESS = 2.0
EFFECT = 2.0


def setup_inputs():
    s = mx_kscale(K)
    t = mx_kscale(F)
    x_words, x_scales = pack4(np.random.standard_normal((K, M)) * s[:, None])
    w_words, w_scales = pack4(STEEPNESS * np.random.standard_normal((K, F)) / np.sqrt(K) / s[:, None])
    v_words, v_scales = pack_weight(EFFECT * np.random.standard_normal((F, N)) / np.sqrt(F) / t[:, None], "e4m3")
    return {"x_words": x_words, "x_scales": x_scales,
            "w_words": w_words, "w_scales": w_scales,
            "rate": bf((1 + 0.1 * np.random.standard_normal(F)) * t),
            "v_words": v_words, "v_scales": v_scales,
            "basal": bf(0.3 * np.random.standard_normal(N)),
            "lifetime": bf(1 + 0.1 * np.random.standard_normal(N))}


def reference(x_words, x_scales, w_words, w_scales, rate, v_words, v_scales, basal, lifetime):
    x = unpack4(x_words, x_scales)
    w = unpack4(w_words, w_scales)
    v = unpack_weight(v_words, v_scales, "e4m3")
    h = x.T @ w
    occ = 1.0 / (1.0 + np.exp(-h))
    act = occ * f64(rate)
    prod = mxq(act, 1, "e4m3") @ v
    return (prod + f64(basal)) * f64(lifetime)

@@ -1,0 +1,323 @@
+from contextlib import ExitStack
+
+import concourse.mybir as mybir
+from concourse.masks import make_identity
+
+M, K, F, N = 1024, 2048, 1024, 1536
+FLOPS = 2 * M * K * F + 2 * M * F * N
+
+F32 = mybir.dt.float32
+BF16 = mybir.dt.bfloat16
+U8 = mybir.dt.uint8
+U32 = mybir.dt.uint32
+I32 = mybir.dt.int32
+FP8X4 = mybir.dt.float8_e4m3fn_x4
+FP4X4 = mybir.dt.float4_e2m1fn_x4
+ACT = mybir.ActivationFunctionType
+ALU = mybir.AluOpType
+
+P = 128
+KG = 4
+FG = 2
+CH = 256
+NCH = M // CH
+NT = 512
+
+ORDER = "q q q q q q q d0 q d0 d0 q q d0 q q d1 d1 d1 d0 q q q q d1 d1 d1 q q q q q d0 d2 p2 q q p2 d2 q d2 T2 d2 d3 p3 p3 d3 T3 d3 d3"
+GP = {(1, 0), (1, 1), (1, 2), (1, 3), (1, 4), (1, 5), (2, 0), (2, 3), (2, 4), (2, 5), (3, 1), (3, 4), (3, 5)}
+ILS = {(2, 0), (2, 1), (3, 0)}
+LADD, LMUL, LSIG, LR0, LR1, LIL, LQ, LEV, LFIN = 1, 4, 1, 3, 3, 3, 4, 2, 2
+
+
+def tile_hill_steady_state_s4_kernel(
+    tc, x_words, x_scales, w_words, w_scales, rate, v_words, v_scales, basal, lifetime, out
+):
+    nc = tc.nc
+    x32 = x_words.bitcast(I32)
+    w32 = w_words.bitcast(I32)
+    v32 = v_words.rearrange("g p n t -> g p (n t)").bitcast(I32)
+    xs32 = x_scales.bitcast(I32).rearrange("k (q r) n -> r q k n", r=4)
+    ws32 = w_scales.bitcast(I32).rearrange("k (q r) n -> r q k n", r=4)
+    vs32 = v_scales.bitcast(I32).rearrange("g (q r) n -> r q g n", r=4)
+
+    with ExitStack() as ctx:
+        keep = ctx.enter_context(tc.tile_pool(name="keep", bufs=1))
+        work = ctx.enter_context(tc.tile_pool(name="work", bufs=2))
+        outs = ctx.enter_context(tc.tile_pool(name="outs", bufs=12))
+        psum = ctx.enter_context(tc.psum_pool(name="psum", bufs=8))
+        ctx.enter_context(tc.manual_schedule())
+
+        xc = [keep.tile([P, KG, 512], U8, align_bytes=64, name=f"xc{c}") for c in range(2)]
+        xc_b = keep.tile([P, KG, 1024], U8, align_bytes=64)
+        wr = [keep.tile([P, KG, 1024], U8, align_bytes=64, name=f"wr{g}") for g in range(FG)]
+        xs = [keep.tile([P, KG, 512], U8, align_bytes=64, name=f"xs{h}") for h in range(2)]
+        wsr = [keep.tile([P, KG, 512], U8, align_bytes=64, name=f"wsr{g}") for g in range(FG)]
+        wp = [[keep.tile([P, 1024], U8, align_bytes=64, name=f"wp{g}_{k}") for k in range(KG)] for g in range(FG)]
+        wsp = [[keep.tile([P, 512], U8, align_bytes=64, name=f"wsp{g}_{k}") for k in range(KG)] for g in range(FG)]
+        vw = keep.tile([P, FG, N], U32, align_bytes=64)
+        vs = keep.tile([P, FG, N], U8, align_bytes=64)
+        rate_bf = keep.tile([P, FG, 4], BF16, align_bytes=64)
+        rate_f = keep.tile([P, FG, 4], F32, align_bytes=64)
+        bas_b = keep.tile([P, N], BF16, align_bytes=64)
+        life_b = keep.tile([P, N], BF16, align_bytes=64)
+        lb_rows = keep.tile([P, 128], BF16, align_bytes=64)
+        lb_cols = keep.tile([P, 128], BF16, align_bytes=64)
+        life_c = keep.tile([P, 4], F32, align_bytes=64)
+        bl_c = keep.tile([P, 4], F32, align_bytes=64)
+        ident = keep.tile([P, P], F32, align_bytes=64)
+        warm = keep.tile([P, 1], F32, align_bytes=64)
+        ac = [[keep.tile([P, CH], U32, align_bytes=64, name=f"ac{c}_{g}") for g in range(FG)] for c in range(NCH)]
+        asc = [[keep.tile([P, CH], U8, align_bytes=64, name=f"as{c}_{g}") for g in range(FG)] for c in range(NCH)]
+
+        def flat32(t):
+            return t[:].rearrange("p k n -> p (k n)").bitcast(I32)
+
+        nc.sync.dma_start(out=wr[0][:, 0, :].bitcast(I32), in_=w32[0, :, 0:256])
+        nc.gpsimd.dma_start(out=xc[0][:].bitcast(I32), in_=x32[:, :, 0:128].rearrange("k p n -> p k n"))
+        nc.vector.memset(flat32(wsr[0]), 0)
+        nc.vector.memset(flat32(xs[0]), 0)
+        nc.vector.memset(warm[:], 0.0)
+        nc.vector.memset(flat32(wsr[1]), 0)
+        nc.vector.memset(flat32(xs[1]), 0)
+        nc.vector.memset(flat32(vs), 0)
+        nc.vector.memset(lb_rows[:], 0.0)
+        nc.scalar.activation(out=warm[:], in_=warm[:], func=ACT.Sigmoid)
+        for r in range(4):
+            nc.sync.dma_start(out=wsr[0][r:128:32, :, :].bitcast(I32), in_=ws32[r, :, :, 0:128])
+        for r in range(4):
+            queue = nc.sync if r < 3 else nc.gpsimd
+            queue.dma_start(out=xs[0][r:128:32, :, :].bitcast(I32), in_=xs32[r, :, :, 0:128])
+        nc.sync.dma_start(out=wr[0][:, 1, :].bitcast(I32), in_=w32[1, :, 0:256])
+        nc.sync.dma_start(out=wr[0][:, 2:4, :].bitcast(I32), in_=w32[2:4, :, 0:256].rearrange("k p n -> p k n"))
+        nc.sync.dma_start(out=rate_bf[:], in_=rate.rearrange("(g p t) -> p g t", p=P, t=4))
+        for r in range(4):
+            nc.sync.dma_start(out=wsr[1][r:128:32, :, :].bitcast(I32), in_=ws32[r, :, :, 128:256])
+        nc.sync.dma_start(out=wr[1][:, 0:2, :].bitcast(I32), in_=w32[0:2, :, 256:512].rearrange("k p n -> p k n"))
+        nc.sync.dma_start(out=wr[1][:, 2:4, :].bitcast(I32), in_=w32[2:4, :, 256:512].rearrange("k p n -> p k n"))
+        nc.sync.dma_start(out=xc[1][:].bitcast(I32), in_=x32[:, :, 128:256].rearrange("k p n -> p k n"))
+        for r in range(4):
+            nc.sync.dma_start(out=vs[r:128:32, :, :].bitcast(I32), in_=vs32[r])
+        for g in range(FG):
+            nc.sync.dma_start(out=vw[:, g, :].bitcast(I32), in_=v32[g])
+        nc.sync.dma_start(out=bas_b[:], in_=basal.partition_broadcast(P))
+        nc.sync.dma_start(out=life_b[:], in_=lifetime.partition_broadcast(P))
+        for r in range(4):
+            nc.sync.dma_start(out=xs[1][r:128:32, :, :].bitcast(I32), in_=xs32[r, :, :, 128:256])
+        nc.sync.dma_start(out=xc_b[:].bitcast(I32), in_=x32[:, :, 256:512].rearrange("k p n -> p k n"))
+        for j in range(4):
+            n0 = 2 * NT + 128 * j
+            nc.gpsimd.dma_start(out=lb_rows[j:128:32, 0:32], in_=lifetime[n0:n0 + 128].rearrange("(a i) -> a i", i=32))
+            nc.gpsimd.dma_start(out=lb_rows[j:128:32, 32:64], in_=basal[n0:n0 + 128].rearrange("(a i) -> a i", i=32))
+        make_identity(nc, ident[:])
+
+        pending = {}
+        clock = [0]
+
+        def at(lag, fn):
+            pending.setdefault(clock[0] + lag, []).append(fn)
+
+        def tick():
+            clock[0] += 1
+            for fn in pending.pop(clock[0], []):
+                fn()
+
+        def permute(g, k):
+            nc.vector.tensor_copy(
+                out=wp[g][k][:].rearrange("p (t m b) -> p t m b", t=4, b=2),
+                in_=wr[g][:, k, :].rearrange("p (m t b) -> p t m b", t=4, b=2),
+            )
+            nc.vector.tensor_copy(
+                out=wsp[g][k][:].rearrange("p (t m) -> p t m", t=4),
+                in_=wsr[g][:, k, :].rearrange("p (m t) -> p t m", t=4),
+            )
+
+        def x_op(k, c):
+            codes = xc[c][:, k, :] if c < 2 else xc_b[:, k, 512 * (c - 2):512 * (c - 1)]
+            h, o = divmod(CH * c, 512)
+            return codes.bitcast(FP4X4), xs[h][:, k, o:o + CH]
+
+        def stage1(bank, g, k, t, c):
+            codes, scales = x_op(k, c)
+            nc.tensor.matmul_mx(
+                out=bank,
+                lhsT=wp[g][k][:, 256 * t:256 * (t + 1)].bitcast(FP4X4),
+                lhsT_scale=wsp[g][k][:, 128 * t:128 * (t + 1)],
+                rhs=codes, rhs_scale=scales,
+                start=(k == 0), stop=(k == KG - 1),
+            )
+
+        def scale_rate(dst, src, g, t):
+            nc.scalar.activation(out=dst, in_=src, func=ACT.Copy, scale=rate_f[:, g, t:t + 1])
+
+        def interleave(c, g, src):
+            a_il = work.tile([P, CH, 4], BF16, align_bytes=64, name="a_il")
+            if (c, g) in ILS:
+                nc.scalar.copy(out=a_il[:], in_=src.rearrange("p t n -> p n t"))
+            else:
+                nc.vector.tensor_copy(out=a_il[:].rearrange("p (n i) t -> p n t i", i=4), in_=src.rearrange("p t (n i) -> p n t i", i=4))
+            return a_il
+
+        def quant(c, g, a_il):
+            nc.vector.quantize_mx(
+                out=ac[c][g][:].bitcast(FP8X4), scales=asc[c][g][:],
+                in_=a_il[:].rearrange("p n t -> p (n t)"),
+            )
+
+        state = {}
+
+        def quarter(c, g, t):
+            if t % 2 == 0:
+                bank = psum.tile([P, 512], F32, name="bank")
+                state["bank"] = bank
+                if t == 0:
+                    occ = work.tile([P, 4, CH], F32, align_bytes=64, name="occ")
+                    act = work.tile([P, 4, CH], BF16, align_bytes=64, name="act")
+                    state["occ"], state["act"] = occ, act
+            bank, occ, act = state["bank"], state["occ"], state["act"]
+            for k in range(KG):
+                stage1(bank[:, CH * (t % 2):CH * (t % 2 + 1)], g, k, t, c)
+
+            def sig():
+                nc.scalar.activation(
+                    out=occ[:, t - 1:t + 1, :].rearrange("p t n -> p (t n)"), in_=bank[:], func=ACT.Sigmoid)
+
+            def rates(ts):
+                for tt in ts:
+                    scale_rate(act[:, tt, :], occ[:, tt, :], g, tt)
+
+            def inter():
+                state[("il", c, g)] = interleave(c, g, act[:])
+
+            if t == 1:
+                at(LSIG, sig)
+            if t == 3:
+                at(LSIG, sig)
+                at(LR0, lambda: rates((0, 1)))
+                at(LR1, lambda: rates((2, 3)))
+                at(LIL, inter)
+                at(LQ, lambda: quant(c, g, state[("il", c, g)]))
+            tick()
+
+        def v_op(g, n0, n):
+            return vw[:, g, n0:n0 + n].bitcast(FP8X4), vs[:, g, n0:n0 + n]
+
+        def a_op(c, g, m0, n):
+            return ac[c][g][:, m0:m0 + n].bitcast(FP8X4), asc[c][g][:, m0:m0 + n]
+
+        def d_tile(c, i, mt, r):
+            bank = psum.tile([P, 512], F32, name="bank")
+            for g in range(FG):
+                a, a_s = a_op(c, g, 128 * mt, 128)
+                v, v_s = v_op(g, NT * r, NT)
+                nc.tensor.matmul_mx(out=bank[:], lhsT=a, lhsT_scale=a_s, rhs=v, rhs_scale=v_s,
+                                    start=(g == 0), stop=(g == FG - 1))
+            o = outs.tile([P, NT], F32, align_bytes=64, name="o")
+            n0 = NT * r
+            m0 = CH * c + 128 * mt
+
+            def add():
+                nc.vector.tensor_tensor(out=o[:], in0=bank[:], in1=bas_b[:, n0:n0 + NT], op=ALU.add)
+
+            def mul():
+                eng = nc.gpsimd if (c, i) in GP else nc.vector
+                eng.tensor_tensor(out=o[:], in0=o[:], in1=life_b[:, n0:n0 + NT], op=ALU.mult)
+                nc.sync.dma_start(out=out[m0:m0 + 128, n0:n0 + NT], in_=o[:])
+
+            at(LADD, add)
+            at(LMUL, mul)
+            tick()
+
+        def p_half(c, i):
+            bank = psum.tile([P, 512], F32, name="bank")
+            if i == 0:
+                p_t = work.tile([P, 4, CH], F32, align_bytes=64, name="p_t")
+                state["p_t", c] = p_t
+            p_t = state["p_t", c]
+            for j in range(2):
+                for g in range(FG):
+                    a, a_s = a_op(c, g, 0, CH)
+                    v, v_s = v_op(g, 2 * NT + 128 * (2 * i + j), 128)
+                    nc.tensor.matmul_mx(out=bank[:, CH * j:CH * (j + 1)], lhsT=v, lhsT_scale=v_s, rhs=a, rhs_scale=a_s,
+                                        start=(g == 0), stop=(g == FG - 1))
+
+            def evac():
+                state["ev", c] = state.get(("ev", c), 0) + 1
+                for j in range(2):
+                    n = 2 * i + j
+                    nc.scalar.activation(out=p_t[:, n, :], in_=bank[:, CH * j:CH * (j + 1)], func=ACT.Identity,
+                                         scale=life_c[:, n:n + 1], bias=bl_c[:, n:n + 1])
+
+            at(LEV, evac)
+            tick()
+
+        def p_turn(c):
+            p_t = state["p_t", c]
+            assert state["ev", c] == 2
+            for mt in range(2):
+                bank = psum.tile([P, 512], F32, name="bank")
+                for j in range(4):
+                    nc.tensor.transpose(bank[:, 128 * j:128 * (j + 1)], p_t[:, j, 128 * mt:128 * (mt + 1)], ident[:])
+                o = outs.tile([P, NT], F32, align_bytes=64, name="o")
+
+                def fin(bank=bank, o=o, m0=CH * c + 128 * mt):
+                    nc.scalar.copy(out=o[:], in_=bank[:])
+                    nc.sync.dma_start(out=out[m0:m0 + 128, 2 * NT:3 * NT], in_=o[:])
+
+                at(LFIN, fin)
+            tick()
+
+        def first_unit(g):
+            banks = []
+            for t in range(4):
+                bank = psum.tile([P, 512], F32, name="bank")
+                banks.append(bank)
+            occ = work.tile([P, 4, CH], F32, align_bytes=64, name="occ")
+            act = work.tile([P, 4, CH], BF16, align_bytes=64, name="act")
+            for k in range(KG):
+                permute(g, k)
+                for t in range(4):
+                    stage1(banks[t][:, 0:CH], g, k, t, 0)
+            for t in range(4):
+                nc.scalar.activation(out=occ[:, t, :], in_=banks[t][:, 0:CH], func=ACT.Sigmoid)
+            if g == 0:
+                nc.vector.tensor_copy(out=rate_f[:].rearrange("p g t -> p (g t)"), in_=rate_bf[:].rearrange("p g t -> p (g t)"))
+            for t in range(4):
+                scale_rate(act[:, t, :], occ[:, t, :], g, t)
+            return act
+
+        act_a = first_unit(0)
+        act_b = first_unit(1)
+        il_a = interleave(0, 0, act_a[:])
+        nc.vector.transpose(lb_cols[:], lb_rows[:])
+        quant(0, 0, il_a)
+        nc.vector.tensor_copy(out=life_c[:], in_=lb_cols[:, 0:4])
+        nc.vector.tensor_tensor(out=bl_c[:], in0=lb_cols[:, 0:4], in1=lb_cols[:, 32:36], op=ALU.mult)
+        il_b = interleave(0, 1, act_b[:])
+        at(1, lambda: quant(0, 1, il_b))
+
+        quarters = []
+        for c in range(1, NCH):
+            for g in range(FG):
+                for t in range(4):
+                    quarters.append((c, g, t))
+        items = ORDER.split()
+        by_p = [f"p{c}" in items for c in range(NCH)]
+        tiles = [[(mt, r) for mt in range(2) for r in range(2 if by_p[c] else 3)] for c in range(NCH)]
+        done = [0] * NCH
+        halves = [0] * NCH
+        for it in items:
+            if it == "q":
+                quarter(*quarters.pop(0))
+                continue
+            c = int(it[1])
+            if it[0] == "d":
+                d_tile(c, done[c], *tiles[c].pop(0))
+                done[c] += 1
+            elif it[0] == "p":
+                p_half(c, halves[c])
+                halves[c] += 1
+            else:
+                p_turn(c)
+        assert not any(tiles) and not quarters
+        for n in range(12):
+            tick()

@@ -23,10 +23,11 @@ CH = 256
 NCH = M // CH
 NT = 512
 
-ORDER = "q q q q q q q d0 q d0 d0 q q d0 q q d1 d1 d1 d0 q q q q d1 d1 d1 q q q q q d0 d2 p2 q q p2 d2 q d2 T2 d2 d3 p3 p3 d3 T3 d3 d3"
-GP = {(1, 0), (1, 1), (1, 2), (1, 3), (1, 4), (1, 5), (2, 0), (2, 3), (2, 4), (2, 5), (3, 1), (3, 4), (3, 5)}
-ILS = {(2, 0), (2, 1), (3, 0)}
-LADD, LMUL, LSIG, LR0, LR1, LIL, LQ, LEV, LFIN = 1, 4, 1, 3, 3, 3, 4, 2, 2
+ORDER = "q q q q q q q q d0 d0 q d0 q q q q d0 d1 q q q d1 d0 q q q q d1 d0 d2 q q q q d2 d1 d1 p2 p2 d2 d1 p3 p3 d3 T2 p3 p3 T3 d2 T3 d3"
+GP = set()
+ILS = {(2, 0), (3, 0), (3, 1)}
+EV = {(0, 0, 1), (0, 1, 0), (1, 0, 0), (1, 1, 1), (1, 2, 1), (2, 0, 0), (2, 1, 1), (3, 0, 1), (3, 1, 0), (3, 1, 1)}
+LADD, LMUL, LSIG, LR0, LR1, LIL, LQ, LEV, LFIN = 1, 3, 1, 1, 1, 5, 6, 1, 1
 
 
 def tile_hill_steady_state_s4_kernel(
@@ -62,8 +63,8 @@ def tile_hill_steady_state_s4_kernel(
         life_b = keep.tile([P, N], BF16, align_bytes=64)
         lb_rows = keep.tile([P, 128], BF16, align_bytes=64)
         lb_cols = keep.tile([P, 128], BF16, align_bytes=64)
-        life_c = keep.tile([P, 4], F32, align_bytes=64)
-        bl_c = keep.tile([P, 4], F32, align_bytes=64)
+        life_c = keep.tile([P, 12], F32, align_bytes=64)
+        bl_c = keep.tile([P, 12], F32, align_bytes=64)
         ident = keep.tile([P, P], F32, align_bytes=64)
         warm = keep.tile([P, 1], F32, align_bytes=64)
         ac = [[keep.tile([P, CH], U32, align_bytes=64, name=f"ac{c}_{g}") for g in range(FG)] for c in range(NCH)]
@@ -104,10 +105,10 @@ def tile_hill_steady_state_s4_kernel(
         for r in range(4):
             nc.sync.dma_start(out=xs[1][r:128:32, :, :].bitcast(I32), in_=xs32[r, :, :, 128:256])
         nc.sync.dma_start(out=xc_b[:].bitcast(I32), in_=x32[:, :, 256:512].rearrange("k p n -> p k n"))
-        for j in range(4):
-            n0 = 2 * NT + 128 * j
-            nc.gpsimd.dma_start(out=lb_rows[j:128:32, 0:32], in_=lifetime[n0:n0 + 128].rearrange("(a i) -> a i", i=32))
-            nc.gpsimd.dma_start(out=lb_rows[j:128:32, 32:64], in_=basal[n0:n0 + 128].rearrange("(a i) -> a i", i=32))
+        for a in range(4):
+            for col, vec in ((0, lifetime), (32, basal)):
+                nc.gpsimd.dma_start(out=lb_rows[32 * a:32 * a + 12, col:col + 32],
+                                    in_=vec.rearrange("(j a i) -> a j i", a=4, i=32)[a])
         make_identity(nc, ident[:])
 
         pending = {}
@@ -227,41 +228,43 @@ def tile_hill_steady_state_s4_kernel(
             at(LMUL, mul)
             tick()
 
-        def p_half(c, i):
+        def p_half(c, r, i):
             bank = psum.tile([P, 512], F32, name="bank")
             if i == 0:
                 p_t = work.tile([P, 4, CH], F32, align_bytes=64, name="p_t")
-                state["p_t", c] = p_t
-            p_t = state["p_t", c]
+                state["p_t", c, r] = p_t
+            p_t = state["p_t", c, r]
             for j in range(2):
                 for g in range(FG):
                     a, a_s = a_op(c, g, 0, CH)
-                    v, v_s = v_op(g, 2 * NT + 128 * (2 * i + j), 128)
+                    v, v_s = v_op(g, NT * r + 128 * (2 * i + j), 128)
                     nc.tensor.matmul_mx(out=bank[:, CH * j:CH * (j + 1)], lhsT=v, lhsT_scale=v_s, rhs=a, rhs_scale=a_s,
                                         start=(g == 0), stop=(g == FG - 1))
 
             def evac():
-                state["ev", c] = state.get(("ev", c), 0) + 1
                 for j in range(2):
                     n = 2 * i + j
+                    q = 4 * r + n
                     nc.scalar.activation(out=p_t[:, n, :], in_=bank[:, CH * j:CH * (j + 1)], func=ACT.Identity,
-                                         scale=life_c[:, n:n + 1], bias=bl_c[:, n:n + 1])
+                                         scale=life_c[:, q:q + 1], bias=bl_c[:, q:q + 1])
 
             at(LEV, evac)
             tick()
 
-        def p_turn(c):
-            p_t = state["p_t", c]
-            assert state["ev", c] == 2
+        def p_turn(c, r):
+            p_t = state["p_t", c, r]
             for mt in range(2):
                 bank = psum.tile([P, 512], F32, name="bank")
                 for j in range(4):
                     nc.tensor.transpose(bank[:, 128 * j:128 * (j + 1)], p_t[:, j, 128 * mt:128 * (mt + 1)], ident[:])
                 o = outs.tile([P, NT], F32, align_bytes=64, name="o")
 
-                def fin(bank=bank, o=o, m0=CH * c + 128 * mt):
-                    nc.scalar.copy(out=o[:], in_=bank[:])
-                    nc.sync.dma_start(out=out[m0:m0 + 128, 2 * NT:3 * NT], in_=o[:])
+                def fin(bank=bank, o=o, m0=CH * c + 128 * mt, v=(c, r, mt) in EV):
+                    if v:
+                        nc.vector.tensor_copy(out=o[:], in_=bank[:])
+                    else:
+                        nc.scalar.copy(out=o[:], in_=bank[:])
+                    nc.sync.dma_start(out=out[m0:m0 + 128, NT * r:NT * (r + 1)], in_=o[:])
 
                 at(LFIN, fin)
             tick()
@@ -290,8 +293,8 @@ def tile_hill_steady_state_s4_kernel(
         il_a = interleave(0, 0, act_a[:])
         nc.vector.transpose(lb_cols[:], lb_rows[:])
         quant(0, 0, il_a)
-        nc.vector.tensor_copy(out=life_c[:], in_=lb_cols[:, 0:4])
-        nc.vector.tensor_tensor(out=bl_c[:], in0=lb_cols[:, 0:4], in1=lb_cols[:, 32:36], op=ALU.mult)
+        nc.vector.tensor_copy(out=life_c[:], in_=lb_cols[:, 0:12])
+        nc.vector.tensor_tensor(out=bl_c[:], in0=lb_cols[:, 0:12], in1=lb_cols[:, 32:44], op=ALU.mult)
         il_b = interleave(0, 1, act_b[:])
         at(1, lambda: quant(0, 1, il_b))
 
@@ -301,10 +304,11 @@ def tile_hill_steady_state_s4_kernel(
                 for t in range(4):
                     quarters.append((c, g, t))
         items = ORDER.split()
-        by_p = [f"p{c}" in items for c in range(NCH)]
-        tiles = [[(mt, r) for mt in range(2) for r in range(2 if by_p[c] else 3)] for c in range(NCH)]
+        n_p = [items.count(f"p{c}") // 2 for c in range(NCH)]
+        tiles = [[(mt, r) for mt in range(2) for r in range(3 - n_p[c])] for c in range(NCH)]
         done = [0] * NCH
         halves = [0] * NCH
+        turns = [0] * NCH
         for it in items:
             if it == "q":
                 quarter(*quarters.pop(0))
@@ -314,10 +318,11 @@ def tile_hill_steady_state_s4_kernel(
                 d_tile(c, done[c], *tiles[c].pop(0))
                 done[c] += 1
             elif it[0] == "p":
-                p_half(c, halves[c])
+                p_half(c, 3 - n_p[c] + halves[c] // 2, halves[c] % 2)
                 halves[c] += 1
             else:
-                p_turn(c)
-        assert not any(tiles) and not quarters
+                p_turn(c, 3 - n_p[c] + turns[c])
+                turns[c] += 1
+        assert not any(tiles) and not quarters and turns == n_p
         for n in range(12):
             tick()

@@ -23,11 +23,12 @@ CH = 256
 NCH = M // CH
 NT = 512
 
-ORDER = "q q q q q q q q d0 d0 q d0 q q q q d0 d1 q q q d1 d0 q q q q d1 d0 d2 q q q q d2 d1 d1 p2 p2 d2 d1 p3 p3 d3 T2 p3 p3 T3 d2 T3 d3"
+ORDER = "q q q q q q d0 q q q q d0 q d0 q d0 q q d0 d0 d1 q q d1 q q q d1 q d1 q p2 q d2 q p2 q p2 d1 p2 T2 T2 d2 d3 p3 d1 p3 p3 p3 T3 T3 d3"
 GP = set()
-ILS = {(2, 0), (3, 0), (3, 1)}
-EV = {(0, 0, 1), (0, 1, 0), (1, 0, 0), (1, 1, 1), (1, 2, 1), (2, 0, 0), (2, 1, 1), (3, 0, 1), (3, 1, 0), (3, 1, 1)}
-LADD, LMUL, LSIG, LR0, LR1, LIL, LQ, LEV, LFIN = 1, 3, 1, 1, 1, 5, 6, 1, 1
+FU = {(0, 0), (0, 1), (1, 1), (3, 1)}
+ILS = set()
+EV = {(0, 0, 0), (0, 2, 0), (0, 2, 1), (1, 0, 0), (1, 1, 1), (2, 0, 1), (2, 2, 0), (3, 0, 0), (3, 1, 0), (3, 2, 0)}
+LADD, LMUL, LSIG, LR0, LR1, LIL, LQ, LEV, LFIN = 1, 4, 1, 1, 1, 3, 6, 2, 1
 
 
 def tile_hill_steady_state_s4_kernel(
@@ -51,12 +52,16 @@ def tile_hill_steady_state_s4_kernel(
         xc = [keep.tile([P, KG, 512], U8, align_bytes=64, name=f"xc{c}") for c in range(2)]
         xc_b = keep.tile([P, KG, 1024], U8, align_bytes=64)
         wr = [keep.tile([P, KG, 1024], U8, align_bytes=64, name=f"wr{g}") for g in range(FG)]
-        xs = [keep.tile([P, KG, 512], U8, align_bytes=64, name=f"xs{h}") for h in range(2)]
-        wsr = [keep.tile([P, KG, 512], U8, align_bytes=64, name=f"wsr{g}") for g in range(FG)]
+        def plane(rows, width, name):
+            t = keep.tile([P, rows * width + 4], U8, align_bytes=64, name=name)
+            return t, t[:, 0:rows * width].rearrange("p (k n) -> p k n", k=rows)
+
+        xs_t, xs = zip(*[plane(KG, w, f"xs{h}") for h, w in enumerate((256, 768))])
+        wsr_t, wsr = zip(*[plane(KG, 512, f"wsr{g}") for g in range(FG)])
         wp = [[keep.tile([P, 1024], U8, align_bytes=64, name=f"wp{g}_{k}") for k in range(KG)] for g in range(FG)]
         wsp = [[keep.tile([P, 512], U8, align_bytes=64, name=f"wsp{g}_{k}") for k in range(KG)] for g in range(FG)]
         vw = keep.tile([P, FG, N], U32, align_bytes=64)
-        vs = keep.tile([P, FG, N], U8, align_bytes=64)
+        vs_t, vs = plane(FG, N, "vs")
         rate_bf = keep.tile([P, FG, 4], BF16, align_bytes=64)
         rate_f = keep.tile([P, FG, 4], F32, align_bytes=64)
         bas_b = keep.tile([P, N], BF16, align_bytes=64)
@@ -66,50 +71,52 @@ def tile_hill_steady_state_s4_kernel(
         life_c = keep.tile([P, 12], F32, align_bytes=64)
         bl_c = keep.tile([P, 12], F32, align_bytes=64)
         ident = keep.tile([P, P], F32, align_bytes=64)
+        ident_b = keep.tile([P, P], BF16, align_bytes=64)
+        zero = keep.tile([P, P], BF16, align_bytes=64)
         warm = keep.tile([P, 1], F32, align_bytes=64)
         ac = [[keep.tile([P, CH], U32, align_bytes=64, name=f"ac{c}_{g}") for g in range(FG)] for c in range(NCH)]
         asc = [[keep.tile([P, CH], U8, align_bytes=64, name=f"as{c}_{g}") for g in range(FG)] for c in range(NCH)]
 
-        def flat32(t):
-            return t[:].rearrange("p k n -> p (k n)").bitcast(I32)
+        def w_load(queue, g, k0, k1):
+            queue.dma_start(out=wr[g][:, k0:k1, :].bitcast(I32),
+                            in_=w32[k0:k1, :, 256 * g:256 * (g + 1)].rearrange("k p n -> p k n"))
 
-        nc.sync.dma_start(out=wr[0][:, 0, :].bitcast(I32), in_=w32[0, :, 0:256])
+        w_load(nc.gpsimd, 0, 0, 2)
         nc.gpsimd.dma_start(out=xc[0][:].bitcast(I32), in_=x32[:, :, 0:128].rearrange("k p n -> p k n"))
-        nc.vector.memset(flat32(wsr[0]), 0)
-        nc.vector.memset(flat32(xs[0]), 0)
+        w_load(nc.gpsimd, 0, 2, 4)
+        w_load(nc.gpsimd, 1, 0, 4)
+        nc.vector.memset(wsr_t[0][:, 0:2048].bitcast(I32), 0)
+        nc.vector.memset(xs_t[0][:, 0:1024].bitcast(I32), 0)
+        nc.vector.memset(zero[:], 0.0)
         nc.vector.memset(warm[:], 0.0)
-        nc.vector.memset(flat32(wsr[1]), 0)
-        nc.vector.memset(flat32(xs[1]), 0)
-        nc.vector.memset(flat32(vs), 0)
+        for t in (wsr_t[1], xs_t[1], vs_t):
+            nc.vector.memset(t[:].bitcast(I32), 0)
         nc.vector.memset(lb_rows[:], 0.0)
         nc.scalar.activation(out=warm[:], in_=warm[:], func=ACT.Sigmoid)
         for r in range(4):
             nc.sync.dma_start(out=wsr[0][r:128:32, :, :].bitcast(I32), in_=ws32[r, :, :, 0:128])
         for r in range(4):
-            queue = nc.sync if r < 3 else nc.gpsimd
-            queue.dma_start(out=xs[0][r:128:32, :, :].bitcast(I32), in_=xs32[r, :, :, 0:128])
-        nc.sync.dma_start(out=wr[0][:, 1, :].bitcast(I32), in_=w32[1, :, 0:256])
-        nc.sync.dma_start(out=wr[0][:, 2:4, :].bitcast(I32), in_=w32[2:4, :, 0:256].rearrange("k p n -> p k n"))
-        nc.sync.dma_start(out=rate_bf[:], in_=rate.rearrange("(g p t) -> p g t", p=P, t=4))
+            nc.sync.dma_start(out=xs[0][r:128:32, :, :].bitcast(I32), in_=xs32[r, :, :, 0:64])
         for r in range(4):
             nc.sync.dma_start(out=wsr[1][r:128:32, :, :].bitcast(I32), in_=ws32[r, :, :, 128:256])
-        nc.sync.dma_start(out=wr[1][:, 0:2, :].bitcast(I32), in_=w32[0:2, :, 256:512].rearrange("k p n -> p k n"))
-        nc.sync.dma_start(out=wr[1][:, 2:4, :].bitcast(I32), in_=w32[2:4, :, 256:512].rearrange("k p n -> p k n"))
-        nc.sync.dma_start(out=xc[1][:].bitcast(I32), in_=x32[:, :, 128:256].rearrange("k p n -> p k n"))
+        nc.sync.dma_start(out=rate_bf[:], in_=rate.rearrange("(g p t) -> p g t", p=P, t=4))
+        for r in range(4):
+            nc.sync.dma_start(out=xs[1][r:128:32, :, :].bitcast(I32), in_=xs32[r, :, :, 64:256])
         for r in range(4):
             nc.sync.dma_start(out=vs[r:128:32, :, :].bitcast(I32), in_=vs32[r])
+        for row, vec in ((0, lifetime), (32, basal)):
+            rows = vec.rearrange("(q p) -> q p", p=P)
+            nc.sync.dma_start(out=lb_rows[row:row + 8, :], in_=rows[0:8])
+            nc.sync.dma_start(out=lb_rows[row + 8:row + 12, :], in_=rows[8:12])
+        nc.sync.dma_start(out=xc[1][:].bitcast(I32), in_=x32[:, :, 128:256].rearrange("k p n -> p k n"))
         for g in range(FG):
             nc.sync.dma_start(out=vw[:, g, :].bitcast(I32), in_=v32[g])
-        nc.sync.dma_start(out=bas_b[:], in_=basal.partition_broadcast(P))
-        nc.sync.dma_start(out=life_b[:], in_=lifetime.partition_broadcast(P))
-        for r in range(4):
-            nc.sync.dma_start(out=xs[1][r:128:32, :, :].bitcast(I32), in_=xs32[r, :, :, 128:256])
         nc.sync.dma_start(out=xc_b[:].bitcast(I32), in_=x32[:, :, 256:512].rearrange("k p n -> p k n"))
-        for a in range(4):
-            for col, vec in ((0, lifetime), (32, basal)):
-                nc.gpsimd.dma_start(out=lb_rows[32 * a:32 * a + 12, col:col + 32],
-                                    in_=vec.rearrange("(j a i) -> a j i", a=4, i=32)[a])
         make_identity(nc, ident[:])
+        nc.sync.dma_start(out=bas_b[:, 0:NT], in_=basal[0:NT].partition_broadcast(P))
+        nc.sync.dma_start(out=life_b[:, 0:NT], in_=lifetime[0:NT].partition_broadcast(P))
+        nc.sync.dma_start(out=bas_b[:, NT:N], in_=basal[NT:N].partition_broadcast(P))
+        nc.sync.dma_start(out=life_b[:, NT:N], in_=lifetime[NT:N].partition_broadcast(P))
 
         pending = {}
         clock = [0]
@@ -134,8 +141,8 @@ def tile_hill_steady_state_s4_kernel(
 
         def x_op(k, c):
             codes = xc[c][:, k, :] if c < 2 else xc_b[:, k, 512 * (c - 2):512 * (c - 1)]
-            h, o = divmod(CH * c, 512)
-            return codes.bitcast(FP4X4), xs[h][:, k, o:o + CH]
+            scales = xs[0][:, k, :] if c == 0 else xs[1][:, k, CH * (c - 1):CH * c]
+            return codes.bitcast(FP4X4), scales
 
         def stage1(bank, g, k, t, c):
             codes, scales = x_op(k, c)
@@ -149,6 +156,13 @@ def tile_hill_steady_state_s4_kernel(
 
         def scale_rate(dst, src, g, t):
             nc.scalar.activation(out=dst, in_=src, func=ACT.Copy, scale=rate_f[:, g, t:t + 1])
+
+        def fused(c, g, occ):
+            a_il = work.tile([P, CH, 4], BF16, align_bytes=64, name="a_il")
+            nc.vector.tensor_tensor(
+                out=a_il[:].rearrange("p (n i) t -> p n t i", i=4), in0=occ.rearrange("p t (n i) -> p n t i", i=4),
+                in1=rate_f[:, g, :].unsqueeze(1).unsqueeze(3).to_broadcast([P, CH // 4, 4, 4]), op=ALU.mult)
+            return a_il
 
         def interleave(c, g, src):
             a_il = work.tile([P, CH, 4], BF16, align_bytes=64, name="a_il")
@@ -187,14 +201,15 @@ def tile_hill_steady_state_s4_kernel(
                     scale_rate(act[:, tt, :], occ[:, tt, :], g, tt)
 
             def inter():
-                state[("il", c, g)] = interleave(c, g, act[:])
+                state[("il", c, g)] = fused(c, g, occ[:]) if (c, g) in FU else interleave(c, g, act[:])
 
             if t == 1:
                 at(LSIG, sig)
             if t == 3:
                 at(LSIG, sig)
-                at(LR0, lambda: rates((0, 1)))
-                at(LR1, lambda: rates((2, 3)))
+                if (c, g) not in FU:
+                    at(LR0, lambda: rates((0, 1)))
+                    at(LR1, lambda: rates((2, 3)))
                 at(LIL, inter)
                 at(LQ, lambda: quant(c, g, state[("il", c, g)]))
             tick()
@@ -226,6 +241,35 @@ def tile_hill_steady_state_s4_kernel(
 
             at(LADD, add)
             at(LMUL, mul)
+            tick()
+
+        def last_tile(c, i, mt, r):
+            o = outs.tile([P, NT], F32, align_bytes=64, name="o")
+            m0 = CH * c + 128 * mt
+            banks = []
+            for h in range(2):
+                bank = psum.tile([P, 512], F32, name="bank")
+                banks.append(bank)
+                for g in range(FG):
+                    a, a_s = a_op(c, g, 128 * mt, 128)
+                    v, v_s = v_op(g, NT * r + 256 * h, 256)
+                    nc.tensor.matmul_mx(out=bank[:, 0:256], lhsT=a, lhsT_scale=a_s, rhs=v, rhs_scale=v_s,
+                                        start=(g == 0), stop=(g == FG - 1))
+
+            def add(h):
+                n0 = NT * r + 256 * h
+                nc.vector.tensor_tensor(out=o[:, 256 * h:256 * (h + 1)], in0=banks[h][:, 0:256], in1=bas_b[:, n0:n0 + 256], op=ALU.add)
+
+            def mul(h):
+                n0 = NT * r + 256 * h
+                oh = o[:, 256 * h:256 * (h + 1)]
+                nc.vector.tensor_tensor(out=oh, in0=oh, in1=life_b[:, n0:n0 + 256], op=ALU.mult)
+                nc.sync.dma_start(out=out[m0:m0 + 128, n0:n0 + 256], in_=oh)
+
+            at(LADD, lambda: add(0))
+            at(LADD, lambda: add(1))
+            at(LMUL, lambda: mul(0))
+            at(LMUL, lambda: mul(1))
             tick()
 
         def p_half(c, r, i):
@@ -269,33 +313,47 @@ def tile_hill_steady_state_s4_kernel(
                 at(LFIN, fin)
             tick()
 
+        cold = psum.tile([P, P], BF16, name="bank")
+        for n in range(28):
+            nc.tensor.transpose(cold[:], zero[:], zero[:])
+
+        def columns():
+            turned = psum.tile([P, P], BF16, name="bank")
+            nc.tensor.transpose(turned[:], lb_rows[:], ident_b[:])
+
+            def finish():
+                nc.scalar.copy(out=lb_cols[:], in_=turned[:])
+                nc.vector.tensor_copy(out=life_c[:], in_=lb_cols[:, 0:12])
+
+            at(1, finish)
+            at(2, lambda: nc.vector.tensor_tensor(out=bl_c[:], in0=lb_cols[:, 0:12], in1=lb_cols[:, 32:44], op=ALU.mult))
+
         def first_unit(g):
             banks = []
             for t in range(4):
                 bank = psum.tile([P, 512], F32, name="bank")
                 banks.append(bank)
             occ = work.tile([P, 4, CH], F32, align_bytes=64, name="occ")
-            act = work.tile([P, 4, CH], BF16, align_bytes=64, name="act")
             for k in range(KG):
                 permute(g, k)
                 for t in range(4):
                     stage1(banks[t][:, 0:CH], g, k, t, 0)
-            for t in range(4):
-                nc.scalar.activation(out=occ[:, t, :], in_=banks[t][:, 0:CH], func=ACT.Sigmoid)
-            if g == 0:
-                nc.vector.tensor_copy(out=rate_f[:].rearrange("p g t -> p (g t)"), in_=rate_bf[:].rearrange("p g t -> p (g t)"))
-            for t in range(4):
-                scale_rate(act[:, t, :], occ[:, t, :], g, t)
-            return act
 
-        act_a = first_unit(0)
-        act_b = first_unit(1)
-        il_a = interleave(0, 0, act_a[:])
-        nc.vector.transpose(lb_cols[:], lb_rows[:])
+            def finish():
+                for t in range(4):
+                    nc.scalar.activation(out=occ[:, t, :], in_=banks[t][:, 0:CH], func=ACT.Sigmoid)
+                if g == 0:
+                    nc.vector.tensor_copy(out=rate_f[:].rearrange("p g t -> p (g t)"), in_=rate_bf[:].rearrange("p g t -> p (g t)"))
+            return occ, finish
+
+        occ_a, finish_a = first_unit(0)
+        nc.vector.tensor_copy(out=ident_b[:], in_=ident[:])
+        finish_a()
+        occ_b, finish_b = first_unit(1)
+        finish_b()
+        il_a = fused(0, 0, occ_a[:])
         quant(0, 0, il_a)
-        nc.vector.tensor_copy(out=life_c[:], in_=lb_cols[:, 0:12])
-        nc.vector.tensor_tensor(out=bl_c[:], in0=lb_cols[:, 0:12], in1=lb_cols[:, 32:44], op=ALU.mult)
-        il_b = interleave(0, 1, act_b[:])
+        il_b = fused(0, 1, occ_b[:])
         at(1, lambda: quant(0, 1, il_b))
 
         quarters = []
@@ -305,17 +363,20 @@ def tile_hill_steady_state_s4_kernel(
                     quarters.append((c, g, t))
         items = ORDER.split()
         n_p = [items.count(f"p{c}") // 2 for c in range(NCH)]
-        tiles = [[(mt, r) for mt in range(2) for r in range(3 - n_p[c])] for c in range(NCH)]
+        tiles = [[(mt, r) for r in range(3 - n_p[c]) for mt in range(2)] for c in range(NCH)]
         done = [0] * NCH
         halves = [0] * NCH
         turns = [0] * NCH
-        for it in items:
+        for n, it in enumerate(items):
+            if n == 8:
+                columns()
             if it == "q":
                 quarter(*quarters.pop(0))
                 continue
             c = int(it[1])
             if it[0] == "d":
-                d_tile(c, done[c], *tiles[c].pop(0))
+                last = c == NCH - 1 and len(tiles[c]) == 1
+                (last_tile if last else d_tile)(c, done[c], *tiles[c].pop(0))
                 done[c] += 1
             elif it[0] == "p":
                 p_half(c, 3 - n_p[c] + halves[c] // 2, halves[c] % 2)

@@ -23,12 +23,14 @@ CH = 256
 NCH = M // CH
 NT = 512
 
-ORDER = "q q q q q q d0 q q q q d0 q d0 q d0 q q d0 d0 d1 q q d1 q q q d1 q d1 q p2 q d2 q p2 q p2 d1 p2 T2 T2 d2 d3 p3 d1 p3 p3 p3 T3 T3 d3"
+ORDER = "q q q q q q d0 q d0 q q d0 q d0 d0 q q d0 q d1 q q q d1 d1 q q q q p1 q d1 p1 q q d2 q p2 p2 d2 T1 T2 d2 d2 p3 p3 d3 p3 p3 T3 T3 d3"
 GP = set()
-FU = {(0, 0), (0, 1), (1, 1), (3, 1)}
-ILS = set()
-EV = {(0, 0, 0), (0, 2, 0), (0, 2, 1), (1, 0, 0), (1, 1, 1), (2, 0, 1), (2, 2, 0), (3, 0, 0), (3, 1, 0), (3, 2, 0)}
-LADD, LMUL, LSIG, LR0, LR1, LIL, LQ, LEV, LFIN = 1, 4, 1, 1, 1, 3, 6, 2, 1
+FU = {(0, 0), (0, 1), (1, 0), (1, 1), (2, 1), (3, 0), (3, 1)}
+JO = {1, 3}
+ILS = {(0, 0), (1, 1), (2, 0), (2, 1)}
+EV = {(0, 0, 0), (0, 0, 1), (0, 1, 1), (0, 2, 0), (0, 2, 1), (1, 0, 0), (1, 0, 1), (1, 1, 1), (2, 1, 0), (2, 1, 1), (3, 0, 1), (3, 1, 0), (3, 2, 0)}
+COLD = 14
+LADD, LMUL, LSIG, LR0, LR1, LIL, LQ, LEV, LFIN = 1, 4, 1, 3, 3, 4, 6, 1, 2
 
 
 def tile_hill_steady_state_s4_kernel(
@@ -45,7 +47,7 @@ def tile_hill_steady_state_s4_kernel(
     with ExitStack() as ctx:
         keep = ctx.enter_context(tc.tile_pool(name="keep", bufs=1))
         work = ctx.enter_context(tc.tile_pool(name="work", bufs=2))
-        outs = ctx.enter_context(tc.tile_pool(name="outs", bufs=12))
+        outs = ctx.enter_context(tc.tile_pool(name="outs", bufs=8))
         psum = ctx.enter_context(tc.psum_pool(name="psum", bufs=8))
         ctx.enter_context(tc.manual_schedule())
 
@@ -59,15 +61,15 @@ def tile_hill_steady_state_s4_kernel(
         xs_t, xs = zip(*[plane(KG, w, f"xs{h}") for h, w in enumerate((256, 768))])
         wsr_t, wsr = zip(*[plane(KG, 512, f"wsr{g}") for g in range(FG)])
         wp = [[keep.tile([P, 1024], U8, align_bytes=64, name=f"wp{g}_{k}") for k in range(KG)] for g in range(FG)]
-        wsp = [[keep.tile([P, 512], U8, align_bytes=64, name=f"wsp{g}_{k}") for k in range(KG)] for g in range(FG)]
+        wsp = [keep.tile([P, KG, 512], U8, align_bytes=64, name=f"wsp{g}") for g in range(FG)]
         vw = keep.tile([P, FG, N], U32, align_bytes=64)
         vs_t, vs = plane(FG, N, "vs")
         rate_bf = keep.tile([P, FG, 4], BF16, align_bytes=64)
         rate_f = keep.tile([P, FG, 4], F32, align_bytes=64)
-        bas_b = keep.tile([P, N], BF16, align_bytes=64)
-        life_b = keep.tile([P, N], BF16, align_bytes=64)
-        lb_rows = keep.tile([P, 128], BF16, align_bytes=64)
-        lb_cols = keep.tile([P, 128], BF16, align_bytes=64)
+        lb_b = keep.tile([P, 2 * N], BF16, align_bytes=64)
+        life_b, bas_b = lb_b[:, 0:N], lb_b[:, N:2 * N]
+        lb_rows = keep.tile([P, 3 * P], BF16, align_bytes=64)
+        lb_cols = keep.tile([P, 3, 64], BF16, align_bytes=64)
         life_c = keep.tile([P, 12], F32, align_bytes=64)
         bl_c = keep.tile([P, 12], F32, align_bytes=64)
         ident = keep.tile([P, P], F32, align_bytes=64)
@@ -81,17 +83,21 @@ def tile_hill_steady_state_s4_kernel(
             queue.dma_start(out=wr[g][:, k0:k1, :].bitcast(I32),
                             in_=w32[k0:k1, :, 256 * g:256 * (g + 1)].rearrange("k p n -> p k n"))
 
-        w_load(nc.gpsimd, 0, 0, 2)
+        nc.vector.memset(lb_rows[:].bitcast(I32), 0)
+        make_identity(nc, ident_b[:])
+        w_load(nc.sync, 0, 0, 2)
+        nc.sync.dma_start(out=lb_rows[0:4, :], in_=lifetime.rearrange("(q n) -> q n", q=4))
+        nc.sync.dma_start(out=lb_rows[32:36, :], in_=basal.rearrange("(q n) -> q n", q=4))
         nc.gpsimd.dma_start(out=xc[0][:].bitcast(I32), in_=x32[:, :, 0:128].rearrange("k p n -> p k n"))
         w_load(nc.gpsimd, 0, 2, 4)
         w_load(nc.gpsimd, 1, 0, 4)
         nc.vector.memset(wsr_t[0][:, 0:2048].bitcast(I32), 0)
         nc.vector.memset(xs_t[0][:, 0:1024].bitcast(I32), 0)
-        nc.vector.memset(zero[:], 0.0)
+        nc.vector.memset(zero[:].bitcast(I32), 0)
         nc.vector.memset(warm[:], 0.0)
-        for t in (wsr_t[1], xs_t[1], vs_t):
-            nc.vector.memset(t[:].bitcast(I32), 0)
-        nc.vector.memset(lb_rows[:], 0.0)
+        nc.vector.memset(wsr_t[1][:].bitcast(I32), 0)
+        nc.vector.memset(xs_t[1][:, 0:3072].bitcast(I32), 0)
+        nc.vector.memset(vs_t[:, 0:3072].bitcast(I32), 0)
         nc.scalar.activation(out=warm[:], in_=warm[:], func=ACT.Sigmoid)
         for r in range(4):
             nc.sync.dma_start(out=wsr[0][r:128:32, :, :].bitcast(I32), in_=ws32[r, :, :, 0:128])
@@ -104,19 +110,11 @@ def tile_hill_steady_state_s4_kernel(
             nc.sync.dma_start(out=xs[1][r:128:32, :, :].bitcast(I32), in_=xs32[r, :, :, 64:256])
         for r in range(4):
             nc.sync.dma_start(out=vs[r:128:32, :, :].bitcast(I32), in_=vs32[r])
-        for row, vec in ((0, lifetime), (32, basal)):
-            rows = vec.rearrange("(q p) -> q p", p=P)
-            nc.sync.dma_start(out=lb_rows[row:row + 8, :], in_=rows[0:8])
-            nc.sync.dma_start(out=lb_rows[row + 8:row + 12, :], in_=rows[8:12])
         nc.sync.dma_start(out=xc[1][:].bitcast(I32), in_=x32[:, :, 128:256].rearrange("k p n -> p k n"))
         for g in range(FG):
             nc.sync.dma_start(out=vw[:, g, :].bitcast(I32), in_=v32[g])
         nc.sync.dma_start(out=xc_b[:].bitcast(I32), in_=x32[:, :, 256:512].rearrange("k p n -> p k n"))
         make_identity(nc, ident[:])
-        nc.sync.dma_start(out=bas_b[:, 0:NT], in_=basal[0:NT].partition_broadcast(P))
-        nc.sync.dma_start(out=life_b[:, 0:NT], in_=lifetime[0:NT].partition_broadcast(P))
-        nc.sync.dma_start(out=bas_b[:, NT:N], in_=basal[NT:N].partition_broadcast(P))
-        nc.sync.dma_start(out=life_b[:, NT:N], in_=lifetime[NT:N].partition_broadcast(P))
 
         pending = {}
         clock = [0]
@@ -134,10 +132,12 @@ def tile_hill_steady_state_s4_kernel(
                 out=wp[g][k][:].rearrange("p (t m b) -> p t m b", t=4, b=2),
                 in_=wr[g][:, k, :].rearrange("p (m t b) -> p t m b", t=4, b=2),
             )
-            nc.vector.tensor_copy(
-                out=wsp[g][k][:].rearrange("p (t m) -> p t m", t=4),
-                in_=wsr[g][:, k, :].rearrange("p (m t) -> p t m", t=4),
-            )
+            k0, n = (k, 1) if g == 0 else (0, KG if k == 0 else 0)
+            if n:
+                nc.vector.tensor_copy(
+                    out=wsp[g][:, k0:k0 + n, :].rearrange("p k (t m) -> p k t m", t=4),
+                    in_=wsr[g][:, k0:k0 + n, :].rearrange("p k (m t) -> p k t m", t=4),
+                )
 
         def x_op(k, c):
             codes = xc[c][:, k, :] if c < 2 else xc_b[:, k, 512 * (c - 2):512 * (c - 1)]
@@ -149,7 +149,7 @@ def tile_hill_steady_state_s4_kernel(
             nc.tensor.matmul_mx(
                 out=bank,
                 lhsT=wp[g][k][:, 256 * t:256 * (t + 1)].bitcast(FP4X4),
-                lhsT_scale=wsp[g][k][:, 128 * t:128 * (t + 1)],
+                lhsT_scale=wsp[g][:, k, 128 * t:128 * (t + 1)],
                 rhs=codes, rhs_scale=scales,
                 start=(k == 0), stop=(k == KG - 1),
             )
@@ -227,24 +227,30 @@ def tile_hill_steady_state_s4_kernel(
                 v, v_s = v_op(g, NT * r, NT)
                 nc.tensor.matmul_mx(out=bank[:], lhsT=a, lhsT_scale=a_s, rhs=v, rhs_scale=v_s,
                                     start=(g == 0), stop=(g == FG - 1))
-            o = outs.tile([P, NT], F32, align_bytes=64, name="o")
             n0 = NT * r
             m0 = CH * c + 128 * mt
+            width = NT * (3 - n_p[c]) if c in JO and (c, mt) != (NCH - 1, 1) else NT
+            if n0 % width == 0:
+                o = outs.tile([P, N], F32, align_bytes=64, name="o")
+                state["o", c, mt] = o
+            o = state["o", c, mt]
+            p0 = n0 % width
 
             def add():
-                nc.vector.tensor_tensor(out=o[:], in0=bank[:], in1=bas_b[:, n0:n0 + NT], op=ALU.add)
+                nc.vector.tensor_tensor(out=o[:, p0:p0 + NT], in0=bank[:], in1=bas_b[:, n0:n0 + NT], op=ALU.add)
 
             def mul():
                 eng = nc.gpsimd if (c, i) in GP else nc.vector
-                eng.tensor_tensor(out=o[:], in0=o[:], in1=life_b[:, n0:n0 + NT], op=ALU.mult)
-                nc.sync.dma_start(out=out[m0:m0 + 128, n0:n0 + NT], in_=o[:])
+                eng.tensor_tensor(out=o[:, 0:width], in0=o[:, 0:width], in1=life_b[:, n0 - p0:n0 - p0 + width], op=ALU.mult)
+                nc.sync.dma_start(out=out[m0:m0 + 128, n0 - p0:n0 - p0 + width], in_=o[:, 0:width])
 
             at(LADD, add)
-            at(LMUL, mul)
+            if p0 + NT == width:
+                at(LMUL, mul)
             tick()
 
         def last_tile(c, i, mt, r):
-            o = outs.tile([P, NT], F32, align_bytes=64, name="o")
+            o = outs.tile([P, NT], F32, align_bytes=64, name="o2")
             m0 = CH * c + 128 * mt
             banks = []
             for h in range(2):
@@ -301,7 +307,7 @@ def tile_hill_steady_state_s4_kernel(
                 bank = psum.tile([P, 512], F32, name="bank")
                 for j in range(4):
                     nc.tensor.transpose(bank[:, 128 * j:128 * (j + 1)], p_t[:, j, 128 * mt:128 * (mt + 1)], ident[:])
-                o = outs.tile([P, NT], F32, align_bytes=64, name="o")
+                o = outs.tile([P, NT], F32, align_bytes=64, name="o2")
 
                 def fin(bank=bank, o=o, m0=CH * c + 128 * mt, v=(c, r, mt) in EV):
                     if v:
@@ -313,20 +319,25 @@ def tile_hill_steady_state_s4_kernel(
                 at(LFIN, fin)
             tick()
 
-        cold = psum.tile([P, P], BF16, name="bank")
-        for n in range(28):
-            nc.tensor.transpose(cold[:], zero[:], zero[:])
+        cold = psum.tile([P, 4 * P], BF16, name="bank")
+        for n in range(COLD):
+            nc.tensor.transpose(cold[:, 3 * P:4 * P], zero[:], zero[:])
+        for j in range(3):
+            nc.tensor.transpose(cold[:, P * j:P * (j + 1)], lb_rows[:, P * j:P * (j + 1)], ident_b[:])
+        nc.scalar.copy(out=lb_cols[:], in_=cold[:, 0:3 * P].rearrange("p (j q) -> p j q", j=3)[:, :, 0:64])
+        for h in range(3):
+            bank = psum.tile([P, 8 * P], BF16, name="bank")
+            for i in range(8):
+                vec, q = divmod(8 * h + i, 12)
+                col = lb_cols[:, q % 3, 32 * vec + q // 3:32 * vec + q // 3 + 1]
+                nc.tensor.transpose(bank[:, P * i:P * (i + 1)], col.to_broadcast([P, P]), ident_b[:])
+            nc.scalar.copy(out=lb_b[:, 8 * P * h:8 * P * (h + 1)], in_=bank[:])
 
         def columns():
-            turned = psum.tile([P, P], BF16, name="bank")
-            nc.tensor.transpose(turned[:], lb_rows[:], ident_b[:])
-
-            def finish():
-                nc.scalar.copy(out=lb_cols[:], in_=turned[:])
-                nc.vector.tensor_copy(out=life_c[:], in_=lb_cols[:, 0:12])
-
-            at(1, finish)
-            at(2, lambda: nc.vector.tensor_tensor(out=bl_c[:], in0=lb_cols[:, 0:12], in1=lb_cols[:, 32:44], op=ALU.mult))
+            life = lb_cols[:, :, 0:4].rearrange("p j r -> p r j")
+            bas = lb_cols[:, :, 32:36].rearrange("p j r -> p r j")
+            nc.vector.tensor_copy(out=life_c[:].rearrange("p (r j) -> p r j", j=3), in_=life)
+            nc.vector.tensor_tensor(out=bl_c[:].rearrange("p (r j) -> p r j", j=3), in0=life, in1=bas, op=ALU.mult)
 
         def first_unit(g):
             banks = []
@@ -347,7 +358,6 @@ def tile_hill_steady_state_s4_kernel(
             return occ, finish
 
         occ_a, finish_a = first_unit(0)
-        nc.vector.tensor_copy(out=ident_b[:], in_=ident[:])
         finish_a()
         occ_b, finish_b = first_unit(1)
         finish_b()
@@ -363,7 +373,7 @@ def tile_hill_steady_state_s4_kernel(
                     quarters.append((c, g, t))
         items = ORDER.split()
         n_p = [items.count(f"p{c}") // 2 for c in range(NCH)]
-        tiles = [[(mt, r) for r in range(3 - n_p[c]) for mt in range(2)] for c in range(NCH)]
+        tiles = [[(mt, r) for mt in range(2) for r in range(3 - n_p[c])] for c in range(NCH)]
         done = [0] * NCH
         halves = [0] * NCH
         turns = [0] * NCH

from contextlib import ExitStack

import concourse.mybir as mybir
from concourse.masks import make_identity

M, K, F, N = 1024, 2048, 1024, 1536
FLOPS = 2 * M * K * F + 2 * M * F * N

F32 = mybir.dt.float32
BF16 = mybir.dt.bfloat16
U8 = mybir.dt.uint8
U32 = mybir.dt.uint32
I32 = mybir.dt.int32
FP8X4 = mybir.dt.float8_e4m3fn_x4
FP4X4 = mybir.dt.float4_e2m1fn_x4
ACT = mybir.ActivationFunctionType
ALU = mybir.AluOpType

P = 128
KG = 4
FG = 2
CH = 256
NCH = M // CH
NT = 512

ORDER = "q q q q q q d0 q d0 q q d0 q d0 d0 q q d0 q d1 q q q d1 d1 q q q q p1 q d1 p1 q q d2 q p2 p2 d2 T1 T2 d2 d2 p3 p3 d3 p3 p3 T3 T3 d3"
GP = set()
FU = {(0, 0), (0, 1), (1, 0), (1, 1), (2, 1), (3, 0), (3, 1)}
JO = {1, 3}
ILS = {(0, 0), (1, 1), (2, 0), (2, 1)}
EV = {(0, 0, 0), (0, 0, 1), (0, 1, 1), (0, 2, 0), (0, 2, 1), (1, 0, 0), (1, 0, 1), (1, 1, 1), (2, 1, 0), (2, 1, 1), (3, 0, 1), (3, 1, 0), (3, 2, 0)}
COLD = 14
LADD, LMUL, LSIG, LR0, LR1, LIL, LQ, LEV, LFIN = 1, 4, 1, 3, 3, 4, 6, 1, 2


def tile_hill_steady_state_s4_kernel(
    tc, x_words, x_scales, w_words, w_scales, rate, v_words, v_scales, basal, lifetime, out
):
    nc = tc.nc
    x32 = x_words.bitcast(I32)
    w32 = w_words.bitcast(I32)
    v32 = v_words.rearrange("g p n t -> g p (n t)").bitcast(I32)
    xs32 = x_scales.bitcast(I32).rearrange("k (q r) n -> r q k n", r=4)
    ws32 = w_scales.bitcast(I32).rearrange("k (q r) n -> r q k n", r=4)
    vs32 = v_scales.bitcast(I32).rearrange("g (q r) n -> r q g n", r=4)

    with ExitStack() as ctx:
        keep = ctx.enter_context(tc.tile_pool(name="keep", bufs=1))
        work = ctx.enter_context(tc.tile_pool(name="work", bufs=2))
        outs = ctx.enter_context(tc.tile_pool(name="outs", bufs=8))
        psum = ctx.enter_context(tc.psum_pool(name="psum", bufs=8))
        ctx.enter_context(tc.manual_schedule())

        xc = [keep.tile([P, KG, 512], U8, align_bytes=64, name=f"xc{c}") for c in range(2)]
        xc_b = keep.tile([P, KG, 1024], U8, align_bytes=64)
        wr = [keep.tile([P, KG, 1024], U8, align_bytes=64, name=f"wr{g}") for g in range(FG)]
        def plane(rows, width, name):
            t = keep.tile([P, rows * width + 4], U8, align_bytes=64, name=name)
            return t, t[:, 0:rows * width].rearrange("p (k n) -> p k n", k=rows)

        xs_t, xs = zip(*[plane(KG, w, f"xs{h}") for h, w in enumerate((256, 768))])
        wsr_t, wsr = zip(*[plane(KG, 512, f"wsr{g}") for g in range(FG)])
        wp = [[keep.tile([P, 1024], U8, align_bytes=64, name=f"wp{g}_{k}") for k in range(KG)] for g in range(FG)]
        wsp = [keep.tile([P, KG, 512], U8, align_bytes=64, name=f"wsp{g}") for g in range(FG)]
        vw = keep.tile([P, FG, N], U32, align_bytes=64)
        vs_t, vs = plane(FG, N, "vs")
        rate_bf = keep.tile([P, FG, 4], BF16, align_bytes=64)
        rate_f = keep.tile([P, FG, 4], F32, align_bytes=64)
        lb_b = keep.tile([P, 2 * N], BF16, align_bytes=64)
        life_b, bas_b = lb_b[:, 0:N], lb_b[:, N:2 * N]
        lb_rows = keep.tile([P, 3 * P], BF16, align_bytes=64)
        lb_cols = keep.tile([P, 3, 64], BF16, align_bytes=64)
        life_c = keep.tile([P, 12], F32, align_bytes=64)
        bl_c = keep.tile([P, 12], F32, align_bytes=64)
        ident = keep.tile([P, P], F32, align_bytes=64)
        ident_b = keep.tile([P, P], BF16, align_bytes=64)
        zero = keep.tile([P, P], BF16, align_bytes=64)
        warm = keep.tile([P, 1], F32, align_bytes=64)
        ac = [[keep.tile([P, CH], U32, align_bytes=64, name=f"ac{c}_{g}") for g in range(FG)] for c in range(NCH)]
        asc = [[keep.tile([P, CH], U8, align_bytes=64, name=f"as{c}_{g}") for g in range(FG)] for c in range(NCH)]

        def w_load(queue, g, k0, k1):
            queue.dma_start(out=wr[g][:, k0:k1, :].bitcast(I32),
                            in_=w32[k0:k1, :, 256 * g:256 * (g + 1)].rearrange("k p n -> p k n"))

        nc.vector.memset(lb_rows[:].bitcast(I32), 0)
        make_identity(nc, ident_b[:])
        w_load(nc.sync, 0, 0, 2)
        nc.sync.dma_start(out=lb_rows[0:4, :], in_=lifetime.rearrange("(q n) -> q n", q=4))
        nc.sync.dma_start(out=lb_rows[32:36, :], in_=basal.rearrange("(q n) -> q n", q=4))
        nc.gpsimd.dma_start(out=xc[0][:].bitcast(I32), in_=x32[:, :, 0:128].rearrange("k p n -> p k n"))
        w_load(nc.gpsimd, 0, 2, 4)
        w_load(nc.gpsimd, 1, 0, 4)
        nc.vector.memset(wsr_t[0][:, 0:2048].bitcast(I32), 0)
        nc.vector.memset(xs_t[0][:, 0:1024].bitcast(I32), 0)
        nc.vector.memset(zero[:].bitcast(I32), 0)
        nc.vector.memset(warm[:], 0.0)
        nc.vector.memset(wsr_t[1][:].bitcast(I32), 0)
        nc.vector.memset(xs_t[1][:, 0:3072].bitcast(I32), 0)
        nc.vector.memset(vs_t[:, 0:3072].bitcast(I32), 0)
        nc.scalar.activation(out=warm[:], in_=warm[:], func=ACT.Sigmoid)
        for r in range(4):
            nc.sync.dma_start(out=wsr[0][r:128:32, :, :].bitcast(I32), in_=ws32[r, :, :, 0:128])
        for r in range(4):
            nc.sync.dma_start(out=xs[0][r:128:32, :, :].bitcast(I32), in_=xs32[r, :, :, 0:64])
        for r in range(4):
            nc.sync.dma_start(out=wsr[1][r:128:32, :, :].bitcast(I32), in_=ws32[r, :, :, 128:256])
        nc.sync.dma_start(out=rate_bf[:], in_=rate.rearrange("(g p t) -> p g t", p=P, t=4))
        for r in range(4):
            nc.sync.dma_start(out=xs[1][r:128:32, :, :].bitcast(I32), in_=xs32[r, :, :, 64:256])
        for r in range(4):
            nc.sync.dma_start(out=vs[r:128:32, :, :].bitcast(I32), in_=vs32[r])
        nc.sync.dma_start(out=xc[1][:].bitcast(I32), in_=x32[:, :, 128:256].rearrange("k p n -> p k n"))
        for g in range(FG):
            nc.sync.dma_start(out=vw[:, g, :].bitcast(I32), in_=v32[g])
        nc.sync.dma_start(out=xc_b[:].bitcast(I32), in_=x32[:, :, 256:512].rearrange("k p n -> p k n"))
        make_identity(nc, ident[:])

        pending = {}
        clock = [0]

        def at(lag, fn):
            pending.setdefault(clock[0] + lag, []).append(fn)

        def tick():
            clock[0] += 1
            for fn in pending.pop(clock[0], []):
                fn()

        def permute(g, k):
            nc.vector.tensor_copy(
                out=wp[g][k][:].rearrange("p (t m b) -> p t m b", t=4, b=2),
                in_=wr[g][:, k, :].rearrange("p (m t b) -> p t m b", t=4, b=2),
            )
            k0, n = (k, 1) if g == 0 else (0, KG if k == 0 else 0)
            if n:
                nc.vector.tensor_copy(
                    out=wsp[g][:, k0:k0 + n, :].rearrange("p k (t m) -> p k t m", t=4),
                    in_=wsr[g][:, k0:k0 + n, :].rearrange("p k (m t) -> p k t m", t=4),
                )

        def x_op(k, c):
            codes = xc[c][:, k, :] if c < 2 else xc_b[:, k, 512 * (c - 2):512 * (c - 1)]
            scales = xs[0][:, k, :] if c == 0 else xs[1][:, k, CH * (c - 1):CH * c]
            return codes.bitcast(FP4X4), scales

        def stage1(bank, g, k, t, c):
            codes, scales = x_op(k, c)
            nc.tensor.matmul_mx(
                out=bank,
                lhsT=wp[g][k][:, 256 * t:256 * (t + 1)].bitcast(FP4X4),
                lhsT_scale=wsp[g][:, k, 128 * t:128 * (t + 1)],
                rhs=codes, rhs_scale=scales,
                start=(k == 0), stop=(k == KG - 1),
            )

        def scale_rate(dst, src, g, t):
            nc.scalar.activation(out=dst, in_=src, func=ACT.Copy, scale=rate_f[:, g, t:t + 1])

        def fused(c, g, occ):
            a_il = work.tile([P, CH, 4], BF16, align_bytes=64, name="a_il")
            nc.vector.tensor_tensor(
                out=a_il[:].rearrange("p (n i) t -> p n t i", i=4), in0=occ.rearrange("p t (n i) -> p n t i", i=4),
                in1=rate_f[:, g, :].unsqueeze(1).unsqueeze(3).to_broadcast([P, CH // 4, 4, 4]), op=ALU.mult)
            return a_il

        def interleave(c, g, src):
            a_il = work.tile([P, CH, 4], BF16, align_bytes=64, name="a_il")
            if (c, g) in ILS:
                nc.scalar.copy(out=a_il[:], in_=src.rearrange("p t n -> p n t"))
            else:
                nc.vector.tensor_copy(out=a_il[:].rearrange("p (n i) t -> p n t i", i=4), in_=src.rearrange("p t (n i) -> p n t i", i=4))
            return a_il

        def quant(c, g, a_il):
            nc.vector.quantize_mx(
                out=ac[c][g][:].bitcast(FP8X4), scales=asc[c][g][:],
                in_=a_il[:].rearrange("p n t -> p (n t)"),
            )

        state = {}

        def quarter(c, g, t):
            if t % 2 == 0:
                bank = psum.tile([P, 512], F32, name="bank")
                state["bank"] = bank
                if t == 0:
                    occ = work.tile([P, 4, CH], F32, align_bytes=64, name="occ")
                    act = work.tile([P, 4, CH], BF16, align_bytes=64, name="act")
                    state["occ"], state["act"] = occ, act
            bank, occ, act = state["bank"], state["occ"], state["act"]
            for k in range(KG):
                stage1(bank[:, CH * (t % 2):CH * (t % 2 + 1)], g, k, t, c)

            def sig():
                nc.scalar.activation(
                    out=occ[:, t - 1:t + 1, :].rearrange("p t n -> p (t n)"), in_=bank[:], func=ACT.Sigmoid)

            def rates(ts):
                for tt in ts:
                    scale_rate(act[:, tt, :], occ[:, tt, :], g, tt)

            def inter():
                state[("il", c, g)] = fused(c, g, occ[:]) if (c, g) in FU else interleave(c, g, act[:])

            if t == 1:
                at(LSIG, sig)
            if t == 3:
                at(LSIG, sig)
                if (c, g) not in FU:
                    at(LR0, lambda: rates((0, 1)))
                    at(LR1, lambda: rates((2, 3)))
                at(LIL, inter)
                at(LQ, lambda: quant(c, g, state[("il", c, g)]))
            tick()

        def v_op(g, n0, n):
            return vw[:, g, n0:n0 + n].bitcast(FP8X4), vs[:, g, n0:n0 + n]

        def a_op(c, g, m0, n):
            return ac[c][g][:, m0:m0 + n].bitcast(FP8X4), asc[c][g][:, m0:m0 + n]

        def d_tile(c, i, mt, r):
            bank = psum.tile([P, 512], F32, name="bank")
            for g in range(FG):
                a, a_s = a_op(c, g, 128 * mt, 128)
                v, v_s = v_op(g, NT * r, NT)
                nc.tensor.matmul_mx(out=bank[:], lhsT=a, lhsT_scale=a_s, rhs=v, rhs_scale=v_s,
                                    start=(g == 0), stop=(g == FG - 1))
            n0 = NT * r
            m0 = CH * c + 128 * mt
            width = NT * (3 - n_p[c]) if c in JO and (c, mt) != (NCH - 1, 1) else NT
            if n0 % width == 0:
                o = outs.tile([P, N], F32, align_bytes=64, name="o")
                state["o", c, mt] = o
            o = state["o", c, mt]
            p0 = n0 % width

            def add():
                nc.vector.tensor_tensor(out=o[:, p0:p0 + NT], in0=bank[:], in1=bas_b[:, n0:n0 + NT], op=ALU.add)

            def mul():
                eng = nc.gpsimd if (c, i) in GP else nc.vector
                eng.tensor_tensor(out=o[:, 0:width], in0=o[:, 0:width], in1=life_b[:, n0 - p0:n0 - p0 + width], op=ALU.mult)
                nc.sync.dma_start(out=out[m0:m0 + 128, n0 - p0:n0 - p0 + width], in_=o[:, 0:width])

            at(LADD, add)
            if p0 + NT == width:
                at(LMUL, mul)
            tick()

        def last_tile(c, i, mt, r):
            o = outs.tile([P, NT], F32, align_bytes=64, name="o2")
            m0 = CH * c + 128 * mt
            banks = []
            for h in range(2):
                bank = psum.tile([P, 512], F32, name="bank")
                banks.append(bank)
                for g in range(FG):
                    a, a_s = a_op(c, g, 128 * mt, 128)
                    v, v_s = v_op(g, NT * r + 256 * h, 256)
                    nc.tensor.matmul_mx(out=bank[:, 0:256], lhsT=a, lhsT_scale=a_s, rhs=v, rhs_scale=v_s,
                                        start=(g == 0), stop=(g == FG - 1))

            def add(h):
                n0 = NT * r + 256 * h
                nc.vector.tensor_tensor(out=o[:, 256 * h:256 * (h + 1)], in0=banks[h][:, 0:256], in1=bas_b[:, n0:n0 + 256], op=ALU.add)

            def mul(h):
                n0 = NT * r + 256 * h
                oh = o[:, 256 * h:256 * (h + 1)]
                nc.vector.tensor_tensor(out=oh, in0=oh, in1=life_b[:, n0:n0 + 256], op=ALU.mult)
                nc.sync.dma_start(out=out[m0:m0 + 128, n0:n0 + 256], in_=oh)

            at(LADD, lambda: add(0))
            at(LADD, lambda: add(1))
            at(LMUL, lambda: mul(0))
            at(LMUL, lambda: mul(1))
            tick()

        def p_half(c, r, i):
            bank = psum.tile([P, 512], F32, name="bank")
            if i == 0:
                p_t = work.tile([P, 4, CH], F32, align_bytes=64, name="p_t")
                state["p_t", c, r] = p_t
            p_t = state["p_t", c, r]
            for j in range(2):
                for g in range(FG):
                    a, a_s = a_op(c, g, 0, CH)
                    v, v_s = v_op(g, NT * r + 128 * (2 * i + j), 128)
                    nc.tensor.matmul_mx(out=bank[:, CH * j:CH * (j + 1)], lhsT=v, lhsT_scale=v_s, rhs=a, rhs_scale=a_s,
                                        start=(g == 0), stop=(g == FG - 1))

            def evac():
                for j in range(2):
                    n = 2 * i + j
                    q = 4 * r + n
                    nc.scalar.activation(out=p_t[:, n, :], in_=bank[:, CH * j:CH * (j + 1)], func=ACT.Identity,
                                         scale=life_c[:, q:q + 1], bias=bl_c[:, q:q + 1])

            at(LEV, evac)
            tick()

        def p_turn(c, r):
            p_t = state["p_t", c, r]
            for mt in range(2):
                bank = psum.tile([P, 512], F32, name="bank")
                for j in range(4):
                    nc.tensor.transpose(bank[:, 128 * j:128 * (j + 1)], p_t[:, j, 128 * mt:128 * (mt + 1)], ident[:])
                o = outs.tile([P, NT], F32, align_bytes=64, name="o2")

                def fin(bank=bank, o=o, m0=CH * c + 128 * mt, v=(c, r, mt) in EV):
                    if v:
                        nc.vector.tensor_copy(out=o[:], in_=bank[:])
                    else:
                        nc.scalar.copy(out=o[:], in_=bank[:])
                    nc.sync.dma_start(out=out[m0:m0 + 128, NT * r:NT * (r + 1)], in_=o[:])

                at(LFIN, fin)
            tick()

        cold = psum.tile([P, 4 * P], BF16, name="bank")
        for n in range(COLD):
            nc.tensor.transpose(cold[:, 3 * P:4 * P], zero[:], zero[:])
        for j in range(3):
            nc.tensor.transpose(cold[:, P * j:P * (j + 1)], lb_rows[:, P * j:P * (j + 1)], ident_b[:])
        nc.scalar.copy(out=lb_cols[:], in_=cold[:, 0:3 * P].rearrange("p (j q) -> p j q", j=3)[:, :, 0:64])
        for h in range(3):
            bank = psum.tile([P, 8 * P], BF16, name="bank")
            for i in range(8):
                vec, q = divmod(8 * h + i, 12)
                col = lb_cols[:, q % 3, 32 * vec + q // 3:32 * vec + q // 3 + 1]
                nc.tensor.transpose(bank[:, P * i:P * (i + 1)], col.to_broadcast([P, P]), ident_b[:])
            nc.scalar.copy(out=lb_b[:, 8 * P * h:8 * P * (h + 1)], in_=bank[:])

        def columns():
            life = lb_cols[:, :, 0:4].rearrange("p j r -> p r j")
            bas = lb_cols[:, :, 32:36].rearrange("p j r -> p r j")
            nc.vector.tensor_copy(out=life_c[:].rearrange("p (r j) -> p r j", j=3), in_=life)
            nc.vector.tensor_tensor(out=bl_c[:].rearrange("p (r j) -> p r j", j=3), in0=life, in1=bas, op=ALU.mult)

        def first_unit(g):
            banks = []
            for t in range(4):
                bank = psum.tile([P, 512], F32, name="bank")
                banks.append(bank)
            occ = work.tile([P, 4, CH], F32, align_bytes=64, name="occ")
            for k in range(KG):
                permute(g, k)
                for t in range(4):
                    stage1(banks[t][:, 0:CH], g, k, t, 0)

            def finish():
                for t in range(4):
                    nc.scalar.activation(out=occ[:, t, :], in_=banks[t][:, 0:CH], func=ACT.Sigmoid)
                if g == 0:
                    nc.vector.tensor_copy(out=rate_f[:].rearrange("p g t -> p (g t)"), in_=rate_bf[:].rearrange("p g t -> p (g t)"))
            return occ, finish

        occ_a, finish_a = first_unit(0)
        finish_a()
        occ_b, finish_b = first_unit(1)
        finish_b()
        il_a = fused(0, 0, occ_a[:])
        quant(0, 0, il_a)
        il_b = fused(0, 1, occ_b[:])
        at(1, lambda: quant(0, 1, il_b))

        quarters = []
        for c in range(1, NCH):
            for g in range(FG):
                for t in range(4):
                    quarters.append((c, g, t))
        items = ORDER.split()
        n_p = [items.count(f"p{c}") // 2 for c in range(NCH)]
        tiles = [[(mt, r) for mt in range(2) for r in range(3 - n_p[c])] for c in range(NCH)]
        done = [0] * NCH
        halves = [0] * NCH
        turns = [0] * NCH
        for n, it in enumerate(items):
            if n == 8:
                columns()
            if it == "q":
                quarter(*quarters.pop(0))
                continue
            c = int(it[1])
            if it[0] == "d":
                last = c == NCH - 1 and len(tiles[c]) == 1
                (last_tile if last else d_tile)(c, done[c], *tiles[c].pop(0))
                done[c] += 1
            elif it[0] == "p":
                p_half(c, 3 - n_p[c] + halves[c] // 2, halves[c] % 2)
                halves[c] += 1
            else:
                p_turn(c, 3 - n_p[c] + turns[c])
                turns[c] += 1
        assert not any(tiles) and not quarters and turns == n_p
        for n in range(12):
            tick()
